import numpy as np
import ml_dtypes


def mxq(x, axis, fmt="e4m3"):
    dtype, down = {"e4m3": (ml_dtypes.float8_e4m3fn, 7), "e5m2": (ml_dtypes.float8_e5m2, 14)}[fmt]
    v = np.moveaxis(np.asarray(x, np.float32).astype(ml_dtypes.bfloat16).astype(np.float64), axis, -1)
    blocks = v.reshape(v.shape[:-1] + (-1, 32))
    amax = np.abs(blocks).max(-1, keepdims=True)
    byte = np.maximum(np.where(amax > 0, np.frexp(amax)[1] - 1 + 127, 0) - down, 1)
    scale = np.exp2(byte - 127.0)
    codes = (blocks / scale).astype(np.float32).astype(dtype).astype(np.float64)
    return np.moveaxis((codes * scale).reshape(v.shape), -1, axis)


WIDE = False


def mx_kscale(k, group=512):
    if not WIDE:
        return np.ones(k)
    levels = np.array([18, -18])
    if group != 512:
        return np.exp2(np.random.permutation(np.resize(levels, k // group))).repeat(group)
    if k % 512:
        return np.exp2(np.random.permutation(np.resize(levels, k // 32))).repeat(32)
    a = np.empty((k // 512, 16))
    for p in range(k // 512):
        a[p, :8] = np.random.permutation(np.resize(levels, 8))
        for g in range(8):
            far = levels[np.abs(levels - a[p, g]) >= 10]
            a[p, g + 8] = far[np.random.randint(len(far))]
    return np.exp2(a.ravel()).repeat(32)


def f64(x):
    return np.asarray(x).astype(np.float64)


G, D, M, N = 8, 128, 128, 512


def setup_inputs():
    n = np.random.standard_normal
    s = mx_kscale(D, 0)[:, None]
    return {
        "x": (n((G, D, N)) * s).astype(np.float32),
        "w": (n((G, D, M)) / np.sqrt(D) / s).astype(np.float32),
        "u": (n((G, D, M)) / np.sqrt(D) / s).astype(np.float32),
        "b": (0.5 * n((G, M, 1))).astype(np.float32),
    }


def reference(x, w, u, b):
    xq = mxq(f64(x), 1, "e4m3")
    h = mxq(f64(w), 1, "e4m3").transpose(0, 2, 1) @ xq
    g = mxq(f64(u), 1, "e4m3").transpose(0, 2, 1) @ xq
    h = h + f64(b)
    y = 1.0 / (1.0 + np.exp(-(h))) * g
    return y

@@ -1,0 +1,149 @@
+from contextlib import ExitStack
+
+import concourse.mybir as mybir
+
+G, D, M, N = 8, 128, 128, 512
+FLOPS = 2 * 2 * G * D * M * N
+
+F32 = mybir.dt.float32
+BF16 = mybir.dt.bfloat16
+U32 = mybir.dt.uint32
+U8 = mybir.dt.uint8
+FP8X4 = mybir.dt.float8_e4m3fn_x4
+ACT = mybir.ActivationFunctionType
+ALU = mybir.AluOpType
+
+P = 128
+PACK = 4
+ROWS = D // PACK
+SIDE = P // ROWS
+SETS = G // SIDE
+RUN = 4
+X_SCALAR_FROM = 384
+HALF = N // 2
+
+
+def tile_rows_gglu_sigmoid_bias_kernel(tc, x, w, u, b, out):
+    nc = tc.nc
+
+    with ExitStack() as ctx:
+        pool = ctx.enter_context(tc.tile_pool(name="sb", bufs=1))
+        psum = ctx.enter_context(tc.psum_pool(name="ps", bufs=1))
+        ctx.enter_context(tc.manual_schedule())
+
+        def operand(name, width):
+            raw = pool.tile([P, PACK, width], F32, name=name + "_raw", align_bytes=64)
+            grouped = pool.tile([P, width, PACK], BF16, name=name + "_bf16", align_bytes=64)
+            codes = pool.tile([P, width], U32, name=name + "_codes", align_bytes=64)
+            scales = pool.tile([P, width], U8, name=name + "_scales", align_bytes=64)
+            return raw, grouped, codes, scales
+
+        xs = [operand("x%d" % s, N) for s in range(SETS)]
+        ws = [operand("w%d" % s, M) for s in range(SETS)]
+        us = [operand("u%d" % s, M) for s in range(SETS)]
+        h_bank = [psum.tile([P, N], F32, name="h%d" % c) for c in range(SIDE)]
+        g_bank = [psum.tile([P, N], F32, name="g%d" % c) for c in range(SIDE)]
+        gate = [pool.tile([P, N], F32, name="gate%d" % g) for g in range(G)]
+        result = [pool.tile([P, N], F32, name="result%d" % g) for g in range(G)]
+        seed = pool.tile([P, 32], F32, name="seed", align_bytes=64)
+        bias_rows = pool.tile([P, 32], F32, name="bias_rows", align_bytes=64)
+        bias = pool.tile([P, 32], F32, name="bias", align_bytes=64)
+
+        def load(op, src, s):
+            rows = src.rearrange("g d n -> (g d) n")[s * SIDE * D : (s + 1) * SIDE * D, :]
+            nc.sync.dma_start(out=op[0][:], in_=rows.rearrange("(p j) n -> p j n", j=PACK))
+
+        def views(op, c0, c1):
+            dst = op[1][:, c0:c1, :].rearrange("p (c i) t -> p c t i", i=RUN)
+            src = op[0][:, :, c0:c1].rearrange("p t (c i) -> p c t i", i=RUN)
+            return dst, src
+
+        def cast_vector(op, c0, c1):
+            dst, src = views(op, c0, c1)
+            nc.vector.tensor_copy(out=dst, in_=src)
+
+        def cast_scalar(op, c0, c1):
+            dst, src = views(op, c0, c1)
+            nc.scalar.copy(out=dst, in_=src)
+
+        def quantise(op, c0, c1):
+            nc.vector.quantize_mx(
+                out=op[2][:, c0:c1].bitcast(FP8X4),
+                scales=op[3][:, c0:c1],
+                in_=op[1][:, c0:c1, :].rearrange("p n t -> p (n t)"),
+            )
+
+        def product(bank, weights, g):
+            s, c = divmod(g, SIDE)
+            rows = slice(c * ROWS, (c + 1) * ROWS)
+            nc.tensor.matmul_mx(
+                out=bank[c][:],
+                lhsT=weights[s][2][rows, :].bitcast(FP8X4),
+                lhsT_scale=weights[s][3][rows, :],
+                rhs=xs[s][2][rows, :].bitcast(FP8X4),
+                rhs_scale=xs[s][3][rows, :],
+                start=True,
+                stop=True,
+            )
+
+        def sigmoid(g):
+            nc.scalar.activation(
+                out=gate[g][:], in_=h_bank[g % SIDE][:], func=ACT.Sigmoid, bias=bias[:, 4 * g : 4 * g + 1]
+            )
+
+        def finish(g):
+            nc.vector.tensor_tensor(out=result[g][:], in0=g_bank[g % SIDE][:], in1=gate[g][:], op=ALU.mult)
+            nc.sync.dma_start(out=out[g], in_=result[g][:])
+
+        for s in range(SETS):
+            load(xs[s], x, s)
+            load(ws[s], w, s)
+            load(us[s], u, s)
+
+        nc.vector.memset(seed[:], 0.0)
+        nc.scalar.activation(out=bias_rows[:], in_=seed[:], func=ACT.Sigmoid)
+        nc.scalar.dma_start(out=bias_rows[0:P:4, :], in_=b.rearrange("g (q i) o -> q g (i o)", q=4))
+
+        cast_vector(xs[0], 0, HALF)
+        cast_vector(xs[0], HALF, X_SCALAR_FROM)
+        cast_scalar(xs[0], X_SCALAR_FROM, N)
+        cast_scalar(ws[0], 0, M)
+        cast_scalar(us[0], 0, M)
+        quantise(xs[0], 0, HALF)
+        quantise(xs[0], HALF, N)
+        quantise(ws[0], 0, M)
+        nc.vector.transpose(out=bias[:], in_=bias_rows[:])
+        quantise(us[0], 0, M)
+        for g in range(SIDE):
+            product(h_bank, ws, g)
+        for g in range(SIDE):
+            product(g_bank, us, g)
+        sigmoid(0)
+        sigmoid(1)
+        finish(0)
+
+        cast_vector(xs[1], 0, HALF)
+        cast_vector(xs[1], HALF, X_SCALAR_FROM)
+        cast_scalar(xs[1], X_SCALAR_FROM, N)
+        cast_scalar(ws[1], 0, M)
+        sigmoid(2)
+        cast_scalar(us[1], 0, M)
+        sigmoid(3)
+        quantise(xs[1], 0, HALF)
+        quantise(xs[1], HALF, N)
+        quantise(ws[1], 0, M)
+        finish(1)
+        finish(2)
+        quantise(us[1], 0, M)
+        finish(3)
+        product(h_bank, ws, 4)
+        product(h_bank, ws, 5)
+        product(h_bank, ws, 6)
+        product(g_bank, us, 4)
+        product(h_bank, ws, 7)
+        product(g_bank, us, 5)
+        product(g_bank, us, 6)
+        product(g_bank, us, 7)
+        for g in range(SIDE, G):
+            sigmoid(g)
+            finish(g)

@@ -86,6 +86,14 @@ def tile_rows_gglu_sigmoid_bias_kernel(tc, x, w, u, b, out):
                 stop=True,
             )
 
+        def products(s):
+            g0 = s * SIDE
+            product(h_bank, ws, g0)
+            for g in range(g0, g0 + SIDE):
+                if g + 1 < g0 + SIDE:
+                    product(h_bank, ws, g + 1)
+                product(g_bank, us, g)
+
         def sigmoid(g):
             nc.scalar.activation(
                 out=gate[g][:], in_=h_bank[g % SIDE][:], func=ACT.Sigmoid, bias=bias[:, 4 * g : 4 * g + 1]
@@ -114,10 +122,7 @@ def tile_rows_gglu_sigmoid_bias_kernel(tc, x, w, u, b, out):
         quantise(ws[0], 0, M)
         nc.vector.transpose(out=bias[:], in_=bias_rows[:])
         quantise(us[0], 0, M)
-        for g in range(SIDE):
-            product(h_bank, ws, g)
-        for g in range(SIDE):
-            product(g_bank, us, g)
+        products(0)
         sigmoid(0)
         sigmoid(1)
         finish(0)
@@ -136,14 +141,7 @@ def tile_rows_gglu_sigmoid_bias_kernel(tc, x, w, u, b, out):
         finish(2)
         quantise(us[1], 0, M)
         finish(3)
-        product(h_bank, ws, 4)
-        product(h_bank, ws, 5)
-        product(h_bank, ws, 6)
-        product(g_bank, us, 4)
-        product(h_bank, ws, 7)
-        product(g_bank, us, 5)
-        product(g_bank, us, 6)
-        product(g_bank, us, 7)
+        products(1)
         for g in range(SIDE, G):
             sigmoid(g)
             finish(g)

@@ -19,7 +19,7 @@ ROWS = D // PACK
 SIDE = P // ROWS
 SETS = G // SIDE
 RUN = 4
-X_SCALAR_FROM = 384
+X_SCALAR_TO = 192
 HALF = N // 2
 
 
@@ -86,62 +86,79 @@ def tile_rows_gglu_sigmoid_bias_kernel(tc, x, w, u, b, out):
                 stop=True,
             )
 
-        def products(s):
-            g0 = s * SIDE
-            product(h_bank, ws, g0)
-            for g in range(g0, g0 + SIDE):
-                if g + 1 < g0 + SIDE:
-                    product(h_bank, ws, g + 1)
-                product(g_bank, us, g)
-
-        def sigmoid(g):
+        def sigmoid(g, c0=0, c1=N):
             nc.scalar.activation(
-                out=gate[g][:], in_=h_bank[g % SIDE][:], func=ACT.Sigmoid, bias=bias[:, 4 * g : 4 * g + 1]
+                out=gate[g][:, c0:c1],
+                in_=h_bank[g % SIDE][:, c0:c1],
+                func=ACT.Sigmoid,
+                bias=bias[:, 4 * g : 4 * g + 1],
             )
 
-        def finish(g):
-            nc.vector.tensor_tensor(out=result[g][:], in0=g_bank[g % SIDE][:], in1=gate[g][:], op=ALU.mult)
-            nc.sync.dma_start(out=out[g], in_=result[g][:])
+        def multiply(g, c0=0, c1=N):
+            nc.vector.tensor_tensor(
+                out=result[g][:, c0:c1], in0=g_bank[g % SIDE][:, c0:c1], in1=gate[g][:, c0:c1], op=ALU.mult
+            )
 
-        for s in range(SETS):
-            load(xs[s], x, s)
-            load(ws[s], w, s)
-            load(us[s], u, s)
+        def store(g, c0=0, c1=N):
+            nc.sync.dma_start(out=out[g][:, c0:c1], in_=result[g][:, c0:c1])
 
         nc.vector.memset(seed[:], 0.0)
         nc.scalar.activation(out=bias_rows[:], in_=seed[:], func=ACT.Sigmoid)
-        nc.scalar.dma_start(out=bias_rows[0:P:4, :], in_=b.rearrange("g (q i) o -> q g (i o)", q=4))
 
-        cast_vector(xs[0], 0, HALF)
-        cast_vector(xs[0], HALF, X_SCALAR_FROM)
-        cast_scalar(xs[0], X_SCALAR_FROM, N)
-        cast_scalar(ws[0], 0, M)
+        load(xs[0], x, 0)
+        load(ws[0], w, 0)
+        load(us[0], u, 0)
+        nc.sync.dma_start(out=bias_rows[0:P:4, :], in_=b.rearrange("g (q i) o -> q g (i o)", q=4))
+        load(ws[1], w, 1)
+        load(xs[1], x, 1)
+        load(us[1], u, 1)
+
+        cast_vector(xs[0], HALF, N)
+        cast_scalar(xs[0], 0, HALF)
+        cast_vector(ws[0], 0, M)
         cast_scalar(us[0], 0, M)
-        quantise(xs[0], 0, HALF)
+        cast_scalar(ws[1], 0, M)
         quantise(xs[0], HALF, N)
         quantise(ws[0], 0, M)
+        quantise(xs[0], 0, HALF)
         nc.vector.transpose(out=bias[:], in_=bias_rows[:])
         quantise(us[0], 0, M)
-        products(0)
-        sigmoid(0)
-        sigmoid(1)
-        finish(0)
-
-        cast_vector(xs[1], 0, HALF)
-        cast_vector(xs[1], HALF, X_SCALAR_FROM)
-        cast_scalar(xs[1], X_SCALAR_FROM, N)
-        cast_scalar(ws[1], 0, M)
-        sigmoid(2)
-        cast_scalar(us[1], 0, M)
-        sigmoid(3)
-        quantise(xs[1], 0, HALF)
-        quantise(xs[1], HALF, N)
         quantise(ws[1], 0, M)
-        finish(1)
-        finish(2)
+        for bank, weights, g in (
+            (h_bank, ws, 0), (h_bank, ws, 1), (g_bank, us, 0), (h_bank, ws, 2),
+            (h_bank, ws, 3), (g_bank, us, 1), (g_bank, us, 2), (g_bank, us, 3),
+        ):
+            product(bank, weights, g)
+        sigmoid(0, 0, HALF)
+        sigmoid(0, HALF, N)
+        multiply(0, 0, HALF)
+        multiply(0, HALF, N)
+        store(0)
+        sigmoid(1)
+
+        cast_vector(xs[1], HALF, N)
+        cast_vector(xs[1], X_SCALAR_TO, HALF)
+        cast_scalar(xs[1], 0, X_SCALAR_TO)
+        cast_scalar(us[1], 0, M)
+        quantise(xs[1], HALF, N)
+        quantise(xs[1], 0, HALF)
+        multiply(1)
+        store(1)
         quantise(us[1], 0, M)
-        finish(3)
-        products(1)
-        for g in range(SIDE, G):
+        for g in (2, 3):
             sigmoid(g)
-            finish(g)
+            multiply(g)
+            store(g)
+        for bank, weights, g in (
+            (h_bank, ws, 4), (h_bank, ws, 5), (h_bank, ws, 6), (g_bank, us, 4),
+            (g_bank, us, 5), (h_bank, ws, 7), (g_bank, us, 6), (g_bank, us, 7),
+        ):
+            product(bank, weights, g)
+        for g in (4, 5, 6):
+            sigmoid(g)
+            multiply(g)
+            store(g)
+        for c0 in (0, HALF):
+            sigmoid(7, c0, c0 + HALF)
+            multiply(7, c0, c0 + HALF)
+            store(7, c0, c0 + HALF)

from contextlib import ExitStack

import concourse.mybir as mybir

G, D, M, N = 8, 128, 128, 512
FLOPS = 2 * 2 * G * D * M * N

F32 = mybir.dt.float32
BF16 = mybir.dt.bfloat16
U32 = mybir.dt.uint32
U8 = mybir.dt.uint8
FP8X4 = mybir.dt.float8_e4m3fn_x4
ACT = mybir.ActivationFunctionType
ALU = mybir.AluOpType

P = 128
PACK = 4
ROWS = D // PACK
SIDE = P // ROWS
SETS = G // SIDE
RUN = 4
X_SCALAR_TO = 192
HALF = N // 2


def tile_rows_gglu_sigmoid_bias_kernel(tc, x, w, u, b, out):
    nc = tc.nc

    with ExitStack() as ctx:
        pool = ctx.enter_context(tc.tile_pool(name="sb", bufs=1))
        psum = ctx.enter_context(tc.psum_pool(name="ps", bufs=1))
        ctx.enter_context(tc.manual_schedule())

        def operand(name, width):
            raw = pool.tile([P, PACK, width], F32, name=name + "_raw", align_bytes=64)
            grouped = pool.tile([P, width, PACK], BF16, name=name + "_bf16", align_bytes=64)
            codes = pool.tile([P, width], U32, name=name + "_codes", align_bytes=64)
            scales = pool.tile([P, width], U8, name=name + "_scales", align_bytes=64)
            return raw, grouped, codes, scales

        xs = [operand("x%d" % s, N) for s in range(SETS)]
        ws = [operand("w%d" % s, M) for s in range(SETS)]
        us = [operand("u%d" % s, M) for s in range(SETS)]
        h_bank = [psum.tile([P, N], F32, name="h%d" % c) for c in range(SIDE)]
        g_bank = [psum.tile([P, N], F32, name="g%d" % c) for c in range(SIDE)]
        gate = [pool.tile([P, N], F32, name="gate%d" % g) for g in range(G)]
        result = [pool.tile([P, N], F32, name="result%d" % g) for g in range(G)]
        seed = pool.tile([P, 32], F32, name="seed", align_bytes=64)
        bias_rows = pool.tile([P, 32], F32, name="bias_rows", align_bytes=64)
        bias = pool.tile([P, 32], F32, name="bias", align_bytes=64)

        def load(op, src, s):
            rows = src.rearrange("g d n -> (g d) n")[s * SIDE * D : (s + 1) * SIDE * D, :]
            nc.sync.dma_start(out=op[0][:], in_=rows.rearrange("(p j) n -> p j n", j=PACK))

        def views(op, c0, c1):
            dst = op[1][:, c0:c1, :].rearrange("p (c i) t -> p c t i", i=RUN)
            src = op[0][:, :, c0:c1].rearrange("p t (c i) -> p c t i", i=RUN)
            return dst, src

        def cast_vector(op, c0, c1):
            dst, src = views(op, c0, c1)
            nc.vector.tensor_copy(out=dst, in_=src)

        def cast_scalar(op, c0, c1):
            dst, src = views(op, c0, c1)
            nc.scalar.copy(out=dst, in_=src)

        def quantise(op, c0, c1):
            nc.vector.quantize_mx(
                out=op[2][:, c0:c1].bitcast(FP8X4),
                scales=op[3][:, c0:c1],
                in_=op[1][:, c0:c1, :].rearrange("p n t -> p (n t)"),
            )

        def product(bank, weights, g):
            s, c = divmod(g, SIDE)
            rows = slice(c * ROWS, (c + 1) * ROWS)
            nc.tensor.matmul_mx(
                out=bank[c][:],
                lhsT=weights[s][2][rows, :].bitcast(FP8X4),
                lhsT_scale=weights[s][3][rows, :],
                rhs=xs[s][2][rows, :].bitcast(FP8X4),
                rhs_scale=xs[s][3][rows, :],
                start=True,
                stop=True,
            )

        def sigmoid(g, c0=0, c1=N):
            nc.scalar.activation(
                out=gate[g][:, c0:c1],
                in_=h_bank[g % SIDE][:, c0:c1],
                func=ACT.Sigmoid,
                bias=bias[:, 4 * g : 4 * g + 1],
            )

        def multiply(g, c0=0, c1=N):
            nc.vector.tensor_tensor(
                out=result[g][:, c0:c1], in0=g_bank[g % SIDE][:, c0:c1], in1=gate[g][:, c0:c1], op=ALU.mult
            )

        def store(g, c0=0, c1=N):
            nc.sync.dma_start(out=out[g][:, c0:c1], in_=result[g][:, c0:c1])

        nc.vector.memset(seed[:], 0.0)
        nc.scalar.activation(out=bias_rows[:], in_=seed[:], func=ACT.Sigmoid)

        load(xs[0], x, 0)
        load(ws[0], w, 0)
        load(us[0], u, 0)
        nc.sync.dma_start(out=bias_rows[0:P:4, :], in_=b.rearrange("g (q i) o -> q g (i o)", q=4))
        load(ws[1], w, 1)
        load(xs[1], x, 1)
        load(us[1], u, 1)

        cast_vector(xs[0], HALF, N)
        cast_scalar(xs[0], 0, HALF)
        cast_vector(ws[0], 0, M)
        cast_scalar(us[0], 0, M)
        cast_scalar(ws[1], 0, M)
        quantise(xs[0], HALF, N)
        quantise(ws[0], 0, M)
        quantise(xs[0], 0, HALF)
        nc.vector.transpose(out=bias[:], in_=bias_rows[:])
        quantise(us[0], 0, M)
        quantise(ws[1], 0, M)
        for bank, weights, g in (
            (h_bank, ws, 0), (h_bank, ws, 1), (g_bank, us, 0), (h_bank, ws, 2),
            (h_bank, ws, 3), (g_bank, us, 1), (g_bank, us, 2), (g_bank, us, 3),
        ):
            product(bank, weights, g)
        sigmoid(0, 0, HALF)
        sigmoid(0, HALF, N)
        multiply(0, 0, HALF)
        multiply(0, HALF, N)
        store(0)
        sigmoid(1)

        cast_vector(xs[1], HALF, N)
        cast_vector(xs[1], X_SCALAR_TO, HALF)
        cast_scalar(xs[1], 0, X_SCALAR_TO)
        cast_scalar(us[1], 0, M)
        quantise(xs[1], HALF, N)
        quantise(xs[1], 0, HALF)
        multiply(1)
        store(1)
        quantise(us[1], 0, M)
        for g in (2, 3):
            sigmoid(g)
            multiply(g)
            store(g)
        for bank, weights, g in (
            (h_bank, ws, 4), (h_bank, ws, 5), (h_bank, ws, 6), (g_bank, us, 4),
            (g_bank, us, 5), (h_bank, ws, 7), (g_bank, us, 6), (g_bank, us, 7),
        ):
            product(bank, weights, g)
        for g in (4, 5, 6):
            sigmoid(g)
            multiply(g)
            store(g)
        for c0 in (0, HALF):
            sigmoid(7, c0, c0 + HALF)
            multiply(7, c0, c0 + HALF)
            store(7, c0, c0 + HALF)
